import numpy as np, ml_dtypes
CORES = [16,32,48,64,80]
N = 5
import mx_ref
NC, G, MB, ROOT = 128, 4, 2, 2
C = np.float32(0.041)
BF = ml_dtypes.bfloat16
def cut(t, i, w=512):
    return t[:, w * i:w * i + w]
def tile(rs):
    return np.stack(rs, axis=2).reshape(128, -1).astype(BF)
def layer(w, X):
    out = []
    for i in range(G):
        for t in range(len(X)):
            p = mx_ref.matmul(mx_ref.quantize(cut(w, len(X) * i + t)), X[t])
            z = p if t == 0 else z + p
        out.append(z)
    return out
def act(Z):
    return [np.maximum(z, 0) * C for z in Z]
def setup_inputs(rng):
    def f(*shape):
        return mx_ref.flush((rng.standard_normal(shape, dtype=np.float32) * np.exp2(rng.integers(-2, 3, shape[:-1] + (1,)))).astype(BF))
    return {"x": f(N, 128, MB * 4 * NC), "w1": f(N, 128, G * 512), "w2": f(N, 128, 512)}
def setup_inputs_blocks(rng):
    d = setup_inputs(rng)
    for k in ("x", "w1", "w2"): d[k] = mx_ref.spread(d[k], rng, 4)
    return d
def setup_inputs_wide(rng):
    d = setup_inputs(rng)
    for k in ("x", "w1", "w2"): d[k] = mx_ref.flush((d[k].astype(np.float32) * np.exp2(rng.integers(-8, 9, (N, 1, 1))).astype(np.float32)).astype(BF))
    return d
def setup_inputs_zeros(rng):
    d = setup_inputs(rng); v = d["x"].reshape(N, 128, -1, 4).copy()
    v[np.broadcast_to((rng.random((N, 1, v.shape[2], 1)) < 0.33), v.shape)] = 0
    d["x"] = v.reshape(d["x"].shape)
    return d
def reference(x, w1, w2):
    H = [mx_ref.quantize(tile(act(layer(w1[ROOT], [mx_ref.quantize(cut(x[ROOT], m, 4 * NC))])))) for m in range(MB)]
    y = np.zeros((N, 128, MB * NC), np.float32)
    for r in range(N):
        qw = mx_ref.quantize(w2[r])
        for m in range(MB):
            y[r][:, NC * m:NC * m + NC] = mx_ref.matmul(qw, H[m])
    return {"y": y}

@@ -1,0 +1,188 @@
+from concourse.bass import DstId, RemoteDMATransfer
+from concourse.mybir import dt, AluOpType, ActivationFunctionType
+
+CORES_SIMULATED = 96
+NB = 4
+MB = 2
+NC = 128
+W = 4 * NC
+BANK = 512
+SCALE = 0.041
+
+SCRATCH = {
+    "xb": ("sbuf", [128, MB * W], "bfloat16"),
+    "w1b": ("sbuf", [128, NB * W], "bfloat16"),
+    "w2b": ("sbuf", [128, W], "bfloat16"),
+    "h": ("sbuf", [128, MB * W], "bfloat16"),
+    "xq": ("sbuf", [128, MB * NC], "float8_e4m3fn_x4"),
+    "xs": ("sbuf", [128, MB * NC], "uint8"),
+    "w1q": ("sbuf", [128, NB * NC], "float8_e4m3fn_x4"),
+    "w1s": ("sbuf", [128, NB * NC], "uint8"),
+    "w2q": ("sbuf", [128, NC], "float8_e4m3fn_x4"),
+    "w2s": ("sbuf", [128, NC], "uint8"),
+    "hq": ("sbuf", [128, MB * NC], "float8_e4m3fn_x4"),
+    "hs": ("sbuf", [128, MB * NC], "uint8"),
+    "ps": ("psum", [128, BANK * NB * MB], "float32"),
+    "yb": ("sbuf", [128, MB * NC], "float32"),
+}
+SEMAPHORES = (["lx0", "lx1", "lwa", "lwb", "lw2", "qx0", "qx1", "qv2", "loc", "rp"]
+              + ["qw%d" % b for b in range(NB)]
+              + ["mm%d%d" % (m, b) for m in range(MB) for b in range(NB)]
+              + ["%s%d" % (s, m) for s in ("act", "qh", "rc", "my", "cp", "st") for m in range(MB)])
+
+
+def engines(mask):
+    return bin(mask).count("1")
+
+
+def plan(T, topo):
+    root = T.cores[T.root]
+    dests = [c for c in T.cores if c != root]
+    near, far = [], []
+    for c in range(CORES_SIMULATED):
+        if c != root and topo.chip(c) == topo.chip(root) and all(topo.may_write(c, d) for d in dests):
+            (near if topo.die(c) == topo.die(root) else far).append(c)
+    p0, p1 = dests[:2], dests[2:]
+    codes = [(far[0], 0, p0), (near[0], 0, p1), (far[1], 1, p1), (near[1], 1, p0)]
+    return root, codes, (far[2], p0), p1
+
+
+def dst_ids(topo, cores):
+    out = []
+    for c in cores:
+        rid, pid, _ = topo.addr(c)
+        out.append(DstId(rid=rid, pnc=pid))
+    return out
+
+
+def codes_of(T, m):
+    return T.hq[:, NC * m:NC * m + NC].bitcast(dt.uint8)
+
+
+def send(topo, me, cores, src, dst, sem, mask=None):
+    if mask is None:
+        mask = topo.mask(me, cores[0])
+        for c in cores:
+            mask &= topo.mask(me, c)
+    return RemoteDMATransfer(dst_ids=dst_ids(topo, cores), dma_engine_mask=mask, remote_sem=sem,
+                             srcs=[src], dsts=[dst for _ in cores]), engines(mask)
+
+
+def last_layer(g, T, waits):
+    A = ActivationFunctionType
+    for m in range(MB):
+        for sem, val in waits[m]:
+            g.tensor.wait_ge(sem, val)
+        cols = slice(NC * m, NC * m + NC)
+        out = T.ps[:, BANK * m:BANK * m + NC]
+        g.tensor.matmul_mx(out, T.w2q[:], T.w2s[:], T.hq[:, cols], T.hs[:, cols], True, True).then_inc(T.sem["my%d" % m], 1)
+    g.vector.wait_ge(T.sem.my0, 1)
+    g.vector.tensor_copy(T.yb[:, 0:NC], T.ps[:, 0:NC]).then_inc(T.sem.cp0, 1)
+    g.scalar.wait_ge(T.sem.my1, 1)
+    g.scalar.activation(T.yb[:, NC:2 * NC], T.ps[:, BANK:BANK + NC], A.Copy).then_inc(T.sem.cp1, 1)
+    g.sync.wait_ge(T.sem.cp0, 1)
+    g.sync.dma_start(T.y[:, 0:NC], T.yb[:, 0:NC]).then_inc(T.sem.st0, 16)
+    g.scalar.wait_ge(T.sem.cp1, 1)
+    g.scalar.dma_start(T.y[:, NC:2 * NC], T.yb[:, NC:2 * NC]).then_inc(T.sem.st1, 16)
+    g.sync.wait_ge(T.sem.st0, 16)
+    g.scalar.wait_ge(T.sem.st1, 16)
+
+
+def root_program(g, core, T, topo, codes, planes, direct):
+    A = ActivationFunctionType
+    s = T.sem
+    half = NB // 2 * W
+    g.sync.dma_start(T.xb[:, 0:W], T.x[:, 0:W]).then_inc(s.lx0, 16)
+    g.scalar.dma_start(T.w1b[:, 0:half], T.w1[:, 0:half]).then_inc(s.lwa, 16)
+    g.sync.dma_start(T.w1b[:, half:2 * half], T.w1[:, half:2 * half]).then_inc(s.lwb, 16)
+    g.sync.dma_start(T.xb[:, W:2 * W], T.x[:, W:2 * W]).then_inc(s.lx1, 16)
+
+    def quant(q, sc, src, i, sem):
+        g.vector.quantize_mx(q[:, NC * i:NC * i + NC], sc[:, NC * i:NC * i + NC], src[:, W * i:W * i + W]).then_inc(sem, 1)
+
+    def product(m, b):
+        g.tensor.matmul_mx(T.ps[:, BANK * (NB * m + b):BANK * (NB * m + b) + NC],
+                           T.w1q[:, NC * b:NC * b + NC], T.w1s[:, NC * b:NC * b + NC],
+                           T.xq[:, NC * m:NC * m + NC], T.xs[:, NC * m:NC * m + NC], True, True).then_inc(s["mm%d%d" % (m, b)], 1)
+
+    def on_scalar(m, b):
+        k = BANK * (NB * m + b)
+        g.scalar.wait_ge(s["mm%d%d" % (m, b)], 1)
+        g.scalar.activation(T.h[:, W * m + b:W * m + W:NB], T.ps[:, k:k + NC], A.Relu, scale=SCALE).then_inc(s["act%d" % m], 1)
+
+    def on_vector(m, b):
+        k = BANK * (NB * m + b)
+        g.vector.wait_ge(s["mm%d%d" % (m, b)], 1)
+        g.vector.tensor_scalar(T.h[:, W * m + b:W * m + W:NB], T.ps[:, k:k + NC], 0.0, SCALE,
+                               AluOpType.max, AluOpType.mult).then_inc(s["act%d" % m], 1)
+
+    for m in range(MB):
+        g.tensor.wait_ge(s["qx%d" % m], 1)
+        for b in range(NB):
+            if m == 0:
+                g.tensor.wait_ge(s["qw%d" % b], 1)
+            product(m, b)
+    g.vector.wait_ge(s.lx0, 16)
+    quant(T.xq, T.xs, T.xb, 0, s.qx0)
+    g.vector.wait_ge(s.lwa, 16)
+    quant(T.w1q, T.w1s, T.w1b, 0, s.qw0)
+    quant(T.w1q, T.w1s, T.w1b, 1, s.qw1)
+    g.vector.wait_ge(s.lwb, 16)
+    quant(T.w1q, T.w1s, T.w1b, 2, s.qw2)
+    quant(T.w1q, T.w1s, T.w1b, 3, s.qw3)
+    on_vector(0, 2)
+    g.vector.wait_ge(s.act0, NB)
+    quant(T.hq, T.hs, T.h, 0, s.qh0)
+    g.vector.wait_ge(s.lx1, 16)
+    quant(T.xq, T.xs, T.xb, 1, s.qx1)
+    on_vector(1, 1)
+    on_vector(1, 3)
+    g.vector.wait_ge(s.act1, NB)
+    quant(T.hq, T.hs, T.h, 1, s.qh1)
+    for m, b in ((0, 0), (0, 1), (0, 3), (1, 0), (1, 2)):
+        on_scalar(m, b)
+    total = 0
+    for m in range(MB):
+        g.wait_ge(s["qh%d" % m], 1)
+        t, n = send(topo, core, [c for c, k, _ in codes if k == m], codes_of(T, m), codes_of(T, m), s["rc%d" % m])
+        g.remote_dma_fused([t], local_sem=s.loc)
+        total += n
+    out = topo.mask(core, direct[0])
+    t0, n0 = send(topo, core, direct, T.hs[:], T.hs[:], s.rp, out)
+    t1, n1 = send(topo, core, [planes[0]], T.hs[:], T.hs[:], s.rp, topo.mask(core, planes[0]) & ~out)
+    g.remote_dma_fused([t0, t1], local_sem=s.loc)
+    total += n0 + n1
+    g.sync.wait_ge(s.qh1, 1)
+    g.sync.dma_start(T.w2b[:], T.w2[:]).then_inc(s.lw2, 16)
+    g.vector.wait_ge(s.lw2, 16)
+    g.vector.quantize_mx(T.w2q[:], T.w2s[:], T.w2b[:]).then_inc(s.qv2, 1)
+    last_layer(g, T, [[(s.qh0, 1), (s.qv2, 1)], [(s.qh1, 1)]])
+    g.wait_ge(s.loc, total)
+
+
+def rank_program(g, core, T, topo):
+    root, codes, planes, direct = plan(T, topo)
+    s = T.sem
+    if core == root:
+        root_program(g, core, T, topo, codes, planes, direct)
+        return
+    for c, m, ranks in codes:
+        if c == core:
+            g.wait_ge(s["rc%d" % m], engines(topo.mask(root, core)))
+            t, n = send(topo, core, ranks, codes_of(T, m), codes_of(T, m), s["rc%d" % m])
+            g.remote_dma_fused([t], local_sem=s.loc)
+            g.wait_ge(s.loc, n)
+            return
+    if core == planes[0]:
+        g.wait_ge(s.rp, engines(topo.mask(root, core) & ~topo.mask(root, direct[0])))
+        t, n = send(topo, core, planes[1], T.hs[:], T.hs[:], s.rp)
+        g.remote_dma_fused([t], local_sem=s.loc)
+        g.wait_ge(s.loc, n)
+        return
+    if T.rank_of(core) is None:
+        return
+    g.sync.dma_start(T.w2b[:], T.w2[:]).then_inc(s.lw2, 16)
+    g.vector.wait_ge(s.lw2, 16)
+    g.vector.quantize_mx(T.w2q[:], T.w2s[:], T.w2b[:]).then_inc(s.qv2, 1)
+    n = engines(topo.mask(root, core))
+    last_layer(g, T, [[(s.qv2, 1), (s.rp, n), (s.rc0, n)], [(s.rc1, n)]])

@@ -8,6 +8,8 @@ NC = 128
 W = 4 * NC
 BANK = 512
 SCALE = 0.041
+HALVES = 2
+PC = NC // HALVES
 
 SCRATCH = {
     "xb": ("sbuf", [128, MB * W], "bfloat16"),
@@ -43,32 +45,28 @@ def plan(T, topo):
         if c != root and topo.chip(c) == topo.chip(root) and all(topo.may_write(c, d) for d in dests):
             (near if topo.die(c) == topo.die(root) else far).append(c)
     p0, p1 = dests[:2], dests[2:]
-    codes = [(far[0], 0, p0), (near[0], 0, p1), (far[1], 1, p1), (near[1], 1, p0)]
-    return root, codes, (far[2], p0), p1
+    return root, [(far[0], 0, p0), (near[0], 1, p0), (far[1], 0, p1), (near[1], 1, p1)], dests
 
 
-def dst_ids(topo, cores):
-    out = []
-    for c in cores:
-        rid, pid, _ = topo.addr(c)
-        out.append(DstId(rid=rid, pnc=pid))
-    return out
+def piece(T, m, i):
+    a = NC * m + PC * i
+    return T.hq[:, a:a + PC].bitcast(dt.uint8)
 
 
-def codes_of(T, m):
-    return T.hq[:, NC * m:NC * m + NC].bitcast(dt.uint8)
-
-
-def send(topo, me, cores, src, dst, sem, mask=None):
+def send(topo, me, cores, src, sem, mask=None):
     if mask is None:
         mask = topo.mask(me, cores[0])
         for c in cores:
             mask &= topo.mask(me, c)
-    return RemoteDMATransfer(dst_ids=dst_ids(topo, cores), dma_engine_mask=mask, remote_sem=sem,
-                             srcs=[src], dsts=[dst for _ in cores]), engines(mask)
+    ids = []
+    for c in cores:
+        rid, pid, _ = topo.addr(c)
+        ids.append(DstId(rid=rid, pnc=pid))
+    return RemoteDMATransfer(dst_ids=ids, dma_engine_mask=mask, remote_sem=sem,
+                             srcs=[src], dsts=[src for _ in cores]), engines(mask)
 
 
-def last_layer(g, T, waits):
+def last_layer(g, T, waits, sent=0):
     A = ActivationFunctionType
     for m in range(MB):
         for sem, val in waits[m]:
@@ -80,6 +78,9 @@ def last_layer(g, T, waits):
     g.vector.tensor_copy(T.yb[:, 0:NC], T.ps[:, 0:NC]).then_inc(T.sem.cp0, 1)
     g.scalar.wait_ge(T.sem.my1, 1)
     g.scalar.activation(T.yb[:, NC:2 * NC], T.ps[:, BANK:BANK + NC], A.Copy).then_inc(T.sem.cp1, 1)
+    if sent:
+        g.sync.wait_ge(T.sem.loc, sent)
+        g.scalar.wait_ge(T.sem.loc, sent)
     g.sync.wait_ge(T.sem.cp0, 1)
     g.sync.dma_start(T.y[:, 0:NC], T.yb[:, 0:NC]).then_inc(T.sem.st0, 16)
     g.scalar.wait_ge(T.sem.cp1, 1)
@@ -88,7 +89,7 @@ def last_layer(g, T, waits):
     g.scalar.wait_ge(T.sem.st1, 16)
 
 
-def root_program(g, core, T, topo, codes, planes, direct):
+def root_program(g, core, T, topo, helpers, dests):
     A = ActivationFunctionType
     s = T.sem
     half = NB // 2 * W
@@ -96,6 +97,8 @@ def root_program(g, core, T, topo, codes, planes, direct):
     g.scalar.dma_start(T.w1b[:, 0:half], T.w1[:, 0:half]).then_inc(s.lwa, 16)
     g.sync.dma_start(T.w1b[:, half:2 * half], T.w1[:, half:2 * half]).then_inc(s.lwb, 16)
     g.sync.dma_start(T.xb[:, W:2 * W], T.x[:, W:2 * W]).then_inc(s.lx1, 16)
+    g.sync.wait_ge(s.lwa, 16)
+    g.sync.dma_start(T.w2b[:], T.w2[:]).then_inc(s.lw2, 16)
 
     def quant(q, sc, src, i, sem):
         g.vector.quantize_mx(q[:, NC * i:NC * i + NC], sc[:, NC * i:NC * i + NC], src[:, W * i:W * i + W]).then_inc(sem, 1)
@@ -130,59 +133,56 @@ def root_program(g, core, T, topo, codes, planes, direct):
     g.vector.wait_ge(s.lwb, 16)
     quant(T.w1q, T.w1s, T.w1b, 2, s.qw2)
     quant(T.w1q, T.w1s, T.w1b, 3, s.qw3)
-    on_vector(0, 2)
-    g.vector.wait_ge(s.act0, NB)
-    quant(T.hq, T.hs, T.h, 0, s.qh0)
     g.vector.wait_ge(s.lx1, 16)
     quant(T.xq, T.xs, T.xb, 1, s.qx1)
+    g.vector.wait_ge(s.act0, NB)
+    quant(T.hq, T.hs, T.h, 0, s.qh0)
     on_vector(1, 1)
     on_vector(1, 3)
     g.vector.wait_ge(s.act1, NB)
     quant(T.hq, T.hs, T.h, 1, s.qh1)
-    for m, b in ((0, 0), (0, 1), (0, 3), (1, 0), (1, 2)):
+    for m, b in ((0, 0), (0, 1), (0, 2), (0, 3), (1, 0), (1, 2)):
         on_scalar(m, b)
+    full = topo.mask(core, helpers[0][0])
+    out = topo.mask(core, dests[0])
+    masks = [out, full & ~out]
     total = 0
     for m in range(MB):
         g.wait_ge(s["qh%d" % m], 1)
-        t, n = send(topo, core, [c for c, k, _ in codes if k == m], codes_of(T, m), codes_of(T, m), s["rc%d" % m])
-        g.remote_dma_fused([t], local_sem=s.loc)
-        total += n
-    out = topo.mask(core, direct[0])
-    t0, n0 = send(topo, core, direct, T.hs[:], T.hs[:], s.rp, out)
-    t1, n1 = send(topo, core, [planes[0]], T.hs[:], T.hs[:], s.rp, topo.mask(core, planes[0]) & ~out)
-    g.remote_dma_fused([t0, t1], local_sem=s.loc)
-    total += n0 + n1
-    g.sync.wait_ge(s.qh1, 1)
-    g.sync.dma_start(T.w2b[:], T.w2[:]).then_inc(s.lw2, 16)
+        both = [send(topo, core, [c for c, i, _ in helpers if i == k], piece(T, m, k), s["rc%d" % m], masks[k]) for k in range(HALVES)]
+        g.remote_dma_fused([t for t, _ in both], local_sem=s.loc)
+        total += sum(n for _, n in both)
+    t, n = send(topo, core, dests, T.hs[:], s.rp)
+    g.remote_dma_fused([t], local_sem=s.loc)
+    total += n
     g.vector.wait_ge(s.lw2, 16)
     g.vector.quantize_mx(T.w2q[:], T.w2s[:], T.w2b[:]).then_inc(s.qv2, 1)
-    last_layer(g, T, [[(s.qh0, 1), (s.qv2, 1)], [(s.qh1, 1)]])
+    last_layer(g, T, [[(s.qh0, 1), (s.qv2, 1)], [(s.qh1, 1)]], total)
     g.wait_ge(s.loc, total)
 
 
 def rank_program(g, core, T, topo):
-    root, codes, planes, direct = plan(T, topo)
+    root, helpers, dests = plan(T, topo)
     s = T.sem
     if core == root:
-        root_program(g, core, T, topo, codes, planes, direct)
+        root_program(g, core, T, topo, helpers, dests)
         return
-    for c, m, ranks in codes:
+    out = topo.mask(root, dests[0])
+    for c, i, ranks in helpers:
         if c == core:
-            g.wait_ge(s["rc%d" % m], engines(topo.mask(root, core)))
-            t, n = send(topo, core, ranks, codes_of(T, m), codes_of(T, m), s["rc%d" % m])
-            g.remote_dma_fused([t], local_sem=s.loc)
-            g.wait_ge(s.loc, n)
+            full = topo.mask(root, core)
+            total = 0
+            for m in range(MB):
+                g.wait_ge(s["rc%d" % m], engines([out, full & ~out][i]))
+                t, n = send(topo, core, ranks, piece(T, m, i), s["rc%d" % m])
+                g.remote_dma_fused([t], local_sem=s.loc)
+                total += n
+            g.wait_ge(s.loc, total)
             return
-    if core == planes[0]:
-        g.wait_ge(s.rp, engines(topo.mask(root, core) & ~topo.mask(root, direct[0])))
-        t, n = send(topo, core, planes[1], T.hs[:], T.hs[:], s.rp)
-        g.remote_dma_fused([t], local_sem=s.loc)
-        g.wait_ge(s.loc, n)
-        return
-    if T.rank_of(core) is None:
+    if core not in dests:
         return
     g.sync.dma_start(T.w2b[:], T.w2[:]).then_inc(s.lw2, 16)
     g.vector.wait_ge(s.lw2, 16)
     g.vector.quantize_mx(T.w2q[:], T.w2s[:], T.w2b[:]).then_inc(s.qv2, 1)
-    n = engines(topo.mask(root, core))
-    last_layer(g, T, [[(s.qv2, 1), (s.rp, n), (s.rc0, n)], [(s.rc1, n)]])
+    n = engines(out)
+    last_layer(g, T, [[(s.qv2, 1), (s.rp, n), (s.rc0, HALVES * n)], [(s.rc1, HALVES * n)]])

from concourse.bass import DstId, RemoteDMATransfer
from concourse.mybir import dt, AluOpType, ActivationFunctionType

CORES_SIMULATED = 96
NB = 4
MB = 2
NC = 128
W = 4 * NC
BANK = 512
SCALE = 0.041
HALVES = 2
PC = NC // HALVES

SCRATCH = {
    "xb": ("sbuf", [128, MB * W], "bfloat16"),
    "w1b": ("sbuf", [128, NB * W], "bfloat16"),
    "w2b": ("sbuf", [128, W], "bfloat16"),
    "h": ("sbuf", [128, MB * W], "bfloat16"),
    "xq": ("sbuf", [128, MB * NC], "float8_e4m3fn_x4"),
    "xs": ("sbuf", [128, MB * NC], "uint8"),
    "w1q": ("sbuf", [128, NB * NC], "float8_e4m3fn_x4"),
    "w1s": ("sbuf", [128, NB * NC], "uint8"),
    "w2q": ("sbuf", [128, NC], "float8_e4m3fn_x4"),
    "w2s": ("sbuf", [128, NC], "uint8"),
    "hq": ("sbuf", [128, MB * NC], "float8_e4m3fn_x4"),
    "hs": ("sbuf", [128, MB * NC], "uint8"),
    "ps": ("psum", [128, BANK * NB * MB], "float32"),
    "yb": ("sbuf", [128, MB * NC], "float32"),
}
SEMAPHORES = (["lx0", "lx1", "lwa", "lwb", "lw2", "qx0", "qx1", "qv2", "loc", "rp"]
              + ["qw%d" % b for b in range(NB)]
              + ["mm%d%d" % (m, b) for m in range(MB) for b in range(NB)]
              + ["%s%d" % (s, m) for s in ("act", "qh", "rc", "my", "cp", "st") for m in range(MB)])


def engines(mask):
    return bin(mask).count("1")


def plan(T, topo):
    root = T.cores[T.root]
    dests = [c for c in T.cores if c != root]
    near, far = [], []
    for c in range(CORES_SIMULATED):
        if c != root and topo.chip(c) == topo.chip(root) and all(topo.may_write(c, d) for d in dests):
            (near if topo.die(c) == topo.die(root) else far).append(c)
    p0, p1 = dests[:2], dests[2:]
    return root, [(far[0], 0, p0), (near[0], 1, p0), (far[1], 0, p1), (near[1], 1, p1)], dests


def piece(T, m, i):
    a = NC * m + PC * i
    return T.hq[:, a:a + PC].bitcast(dt.uint8)


def send(topo, me, cores, src, sem, mask=None):
    if mask is None:
        mask = topo.mask(me, cores[0])
        for c in cores:
            mask &= topo.mask(me, c)
    ids = []
    for c in cores:
        rid, pid, _ = topo.addr(c)
        ids.append(DstId(rid=rid, pnc=pid))
    return RemoteDMATransfer(dst_ids=ids, dma_engine_mask=mask, remote_sem=sem,
                             srcs=[src], dsts=[src for _ in cores]), engines(mask)


def last_layer(g, T, waits, sent=0):
    A = ActivationFunctionType
    for m in range(MB):
        for sem, val in waits[m]:
            g.tensor.wait_ge(sem, val)
        cols = slice(NC * m, NC * m + NC)
        out = T.ps[:, BANK * m:BANK * m + NC]
        g.tensor.matmul_mx(out, T.w2q[:], T.w2s[:], T.hq[:, cols], T.hs[:, cols], True, True).then_inc(T.sem["my%d" % m], 1)
    g.vector.wait_ge(T.sem.my0, 1)
    g.vector.tensor_copy(T.yb[:, 0:NC], T.ps[:, 0:NC]).then_inc(T.sem.cp0, 1)
    g.scalar.wait_ge(T.sem.my1, 1)
    g.scalar.activation(T.yb[:, NC:2 * NC], T.ps[:, BANK:BANK + NC], A.Copy).then_inc(T.sem.cp1, 1)
    if sent:
        g.sync.wait_ge(T.sem.loc, sent)
        g.scalar.wait_ge(T.sem.loc, sent)
    g.sync.wait_ge(T.sem.cp0, 1)
    g.sync.dma_start(T.y[:, 0:NC], T.yb[:, 0:NC]).then_inc(T.sem.st0, 16)
    g.scalar.wait_ge(T.sem.cp1, 1)
    g.scalar.dma_start(T.y[:, NC:2 * NC], T.yb[:, NC:2 * NC]).then_inc(T.sem.st1, 16)
    g.sync.wait_ge(T.sem.st0, 16)
    g.scalar.wait_ge(T.sem.st1, 16)


def root_program(g, core, T, topo, helpers, dests):
    A = ActivationFunctionType
    s = T.sem
    half = NB // 2 * W
    g.sync.dma_start(T.xb[:, 0:W], T.x[:, 0:W]).then_inc(s.lx0, 16)
    g.scalar.dma_start(T.w1b[:, 0:half], T.w1[:, 0:half]).then_inc(s.lwa, 16)
    g.sync.dma_start(T.w1b[:, half:2 * half], T.w1[:, half:2 * half]).then_inc(s.lwb, 16)
    g.sync.dma_start(T.xb[:, W:2 * W], T.x[:, W:2 * W]).then_inc(s.lx1, 16)
    g.sync.wait_ge(s.lwa, 16)
    g.sync.dma_start(T.w2b[:], T.w2[:]).then_inc(s.lw2, 16)

    def quant(q, sc, src, i, sem):
        g.vector.quantize_mx(q[:, NC * i:NC * i + NC], sc[:, NC * i:NC * i + NC], src[:, W * i:W * i + W]).then_inc(sem, 1)

    def product(m, b):
        g.tensor.matmul_mx(T.ps[:, BANK * (NB * m + b):BANK * (NB * m + b) + NC],
                           T.w1q[:, NC * b:NC * b + NC], T.w1s[:, NC * b:NC * b + NC],
                           T.xq[:, NC * m:NC * m + NC], T.xs[:, NC * m:NC * m + NC], True, True).then_inc(s["mm%d%d" % (m, b)], 1)

    def on_scalar(m, b):
        k = BANK * (NB * m + b)
        g.scalar.wait_ge(s["mm%d%d" % (m, b)], 1)
        g.scalar.activation(T.h[:, W * m + b:W * m + W:NB], T.ps[:, k:k + NC], A.Relu, scale=SCALE).then_inc(s["act%d" % m], 1)

    def on_vector(m, b):
        k = BANK * (NB * m + b)
        g.vector.wait_ge(s["mm%d%d" % (m, b)], 1)
        g.vector.tensor_scalar(T.h[:, W * m + b:W * m + W:NB], T.ps[:, k:k + NC], 0.0, SCALE,
                               AluOpType.max, AluOpType.mult).then_inc(s["act%d" % m], 1)

    for m in range(MB):
        g.tensor.wait_ge(s["qx%d" % m], 1)
        for b in range(NB):
            if m == 0:
                g.tensor.wait_ge(s["qw%d" % b], 1)
            product(m, b)
    g.vector.wait_ge(s.lx0, 16)
    quant(T.xq, T.xs, T.xb, 0, s.qx0)
    g.vector.wait_ge(s.lwa, 16)
    quant(T.w1q, T.w1s, T.w1b, 0, s.qw0)
    quant(T.w1q, T.w1s, T.w1b, 1, s.qw1)
    g.vector.wait_ge(s.lwb, 16)
    quant(T.w1q, T.w1s, T.w1b, 2, s.qw2)
    quant(T.w1q, T.w1s, T.w1b, 3, s.qw3)
    g.vector.wait_ge(s.lx1, 16)
    quant(T.xq, T.xs, T.xb, 1, s.qx1)
    g.vector.wait_ge(s.act0, NB)
    quant(T.hq, T.hs, T.h, 0, s.qh0)
    on_vector(1, 1)
    on_vector(1, 3)
    g.vector.wait_ge(s.act1, NB)
    quant(T.hq, T.hs, T.h, 1, s.qh1)
    for m, b in ((0, 0), (0, 1), (0, 2), (0, 3), (1, 0), (1, 2)):
        on_scalar(m, b)
    full = topo.mask(core, helpers[0][0])
    out = topo.mask(core, dests[0])
    masks = [out, full & ~out]
    total = 0
    for m in range(MB):
        g.wait_ge(s["qh%d" % m], 1)
        both = [send(topo, core, [c for c, i, _ in helpers if i == k], piece(T, m, k), s["rc%d" % m], masks[k]) for k in range(HALVES)]
        g.remote_dma_fused([t for t, _ in both], local_sem=s.loc)
        total += sum(n for _, n in both)
    t, n = send(topo, core, dests, T.hs[:], s.rp)
    g.remote_dma_fused([t], local_sem=s.loc)
    total += n
    g.vector.wait_ge(s.lw2, 16)
    g.vector.quantize_mx(T.w2q[:], T.w2s[:], T.w2b[:]).then_inc(s.qv2, 1)
    last_layer(g, T, [[(s.qh0, 1), (s.qv2, 1)], [(s.qh1, 1)]], total)
    g.wait_ge(s.loc, total)


def rank_program(g, core, T, topo):
    root, helpers, dests = plan(T, topo)
    s = T.sem
    if core == root:
        root_program(g, core, T, topo, helpers, dests)
        return
    out = topo.mask(root, dests[0])
    for c, i, ranks in helpers:
        if c == core:
            full = topo.mask(root, core)
            total = 0
            for m in range(MB):
                g.wait_ge(s["rc%d" % m], engines([out, full & ~out][i]))
                t, n = send(topo, core, ranks, piece(T, m, i), s["rc%d" % m])
                g.remote_dma_fused([t], local_sem=s.loc)
                total += n
            g.wait_ge(s.loc, total)
            return
    if core not in dests:
        return
    g.sync.dma_start(T.w2b[:], T.w2[:]).then_inc(s.lw2, 16)
    g.vector.wait_ge(s.lw2, 16)
    g.vector.quantize_mx(T.w2q[:], T.w2s[:], T.w2b[:]).then_inc(s.qv2, 1)
    n = engines(out)
    last_layer(g, T, [[(s.qv2, 1), (s.rp, n), (s.rc0, HALVES * n)], [(s.rc1, HALVES * n)]])
